import numpy as np
import ml_dtypes


def mxq(x, axis, fmt="e4m3"):
    dtype, down = {"e4m3": (ml_dtypes.float8_e4m3fn, 7), "e5m2": (ml_dtypes.float8_e5m2, 14)}[fmt]
    v = np.moveaxis(np.asarray(x, np.float32).astype(ml_dtypes.bfloat16).astype(np.float64), axis, -1)
    blocks = v.reshape(v.shape[:-1] + (-1, 32))
    amax = np.abs(blocks).max(-1, keepdims=True)
    byte = np.maximum(np.where(amax > 0, np.frexp(amax)[1] - 1 + 127, 0) - down, 1)
    scale = np.exp2(byte - 127.0)
    codes = (blocks / scale).astype(np.float32).astype(dtype).astype(np.float64)
    return np.moveaxis((codes * scale).reshape(v.shape), -1, axis)


WIDE = False


def mx_kscale(k):
    if not WIDE:
        return np.ones(k)
    levels = np.array([10, -10, 5, -5, 0])
    if k % 512:
        return np.exp2(np.random.permutation(np.resize(levels, k // 32))).repeat(32)
    a = np.empty((k // 512, 16))
    for p in range(k // 512):
        a[p, :8] = np.random.permutation(np.resize(levels, 8))
        for g in range(8):
            far = levels[np.abs(levels - a[p, g]) >= 10]
            a[p, g + 8] = far[np.random.randint(len(far))]
    return np.exp2(a.ravel()).repeat(32)


def f64(x):
    return np.asarray(x).astype(np.float64)


def striped(idx):
    return np.tile(idx.reshape(-1, 16).T, (8, 1)).astype(np.uint16)


def unstriped(offs):
    return offs[:16].T.reshape(-1).astype(np.int64)


E2M1 = np.array([0.0, 0.5, 1.0, 1.5, 2.0, 3.0, 4.0, 6.0, -0.0, -0.5, -1.0, -1.5, -2.0, -3.0, -4.0, -6.0])


def pack_weight(w, fmt):
    k, n = w.shape
    w = f64(np.asarray(w, np.float32).astype(ml_dtypes.bfloat16)).reshape(k // 32, 32, n)
    amax = np.abs(w).max(1)
    if fmt == "e4m3":
        byte = np.frexp(amax)[1] - 1 + 127 - 7
    else:
        mant, ex = np.frexp(amax / 6.0)
        byte = np.where(mant > 0.5, ex, ex - 1) + 127
    byte = np.clip(np.where(amax > 0, byte, 1), 1, 254)
    scaled = (w * np.exp2(127.0 - byte)[:, None, :]).reshape(k, n).astype(np.float32)
    by_word = np.ascontiguousarray(scaled.reshape(k // 512, 128, 4, n).transpose(0, 1, 3, 2))
    if fmt == "e4m3":
        words = by_word.astype(ml_dtypes.float8_e4m3fn).view(np.uint8)
    else:
        c = by_word.astype(ml_dtypes.float4_e2m1fn).view(np.uint8) & 0xF
        words = (c[..., 0::2] | (c[..., 1::2] << 4)).reshape(k // 512, 128, 2 * n)
    return np.ascontiguousarray(words), np.ascontiguousarray(byte.astype(np.uint8).reshape(k // 512, 16, n))


def unpack_weight(words, scales, fmt):
    g, _, n = scales.shape
    words = np.ascontiguousarray(words).reshape(g, 128, n, -1)
    if fmt == "e4m3":
        vals = words.view(ml_dtypes.float8_e4m3fn).astype(np.float64)
    else:
        nib = np.empty((g, 128, n, 4), np.uint8)
        nib[..., 0::2] = words & 0xF
        nib[..., 1::2] = words >> 4
        vals = E2M1[nib]
    vals = vals * np.repeat(np.exp2(scales.astype(np.float64) - 127.0), 8, axis=1)[..., None]
    return vals.transpose(0, 1, 3, 2).reshape(g * 512, n)


def gelu(v):
    return 0.5 * v * (1.0 + np.tanh(np.sqrt(2.0 / np.pi) * (v + 0.044715 * v**3)))


K, T, H, S, T2, P, M, N = 1024, 2048, 512, 512, 1024, 256, 512, 512

def setup_inputs():
    n = np.random.standard_normal
    s = mx_kscale(K)[:, None]
    u = mx_kscale(H)[:, None]
    f = mx_kscale(M)[:, None]
    tab_words, tab_scales = pack_weight(n((K, T)) * s, "e4m3")
    w1_words, w1_scales = pack_weight(1.2 * n((K, H)) / np.sqrt(K) / s, "e2m1")
    w2 = (0.55 * n((K, H)) / np.sqrt(K) / s).astype(np.float32)
    gain = (np.exp(0.3 * n(H)) * u[:, 0]).astype(np.float32)
    wgs = np.exp(0.3 * n((128, S))).astype(np.float32)
    page0 = (0.6 * n((H, T2)) * u).astype(np.float32)
    swap = (0.8 * n(H)).astype(np.float32)
    wo = (n((H, N)) / np.sqrt(H) / u).astype(np.float32)
    fix = (n((M, T2)) * f).astype(np.float32)
    wf_words, wf_scales = pack_weight(0.5 * n((M, N)) / np.sqrt(M) / f, "e4m3")
    perm = np.random.permutation(T2)
    return dict(tab_words=tab_words, tab_scales=tab_scales, offs=striped(np.random.permutation(T)[:S]),
                w1_words=w1_words, w1_scales=w1_scales, w2=w2, gain=gain, wgs=wgs, page0=page0,
                offs2=striped(np.random.permutation(T2)[:S]), offs3=striped(perm[:P]), offs4=striped(perm[P:2 * P]),
                swap=swap, wo=wo, fix=fix, wf_words=wf_words, wf_scales=wf_scales)

def reference(tab_words, tab_scales, offs, w1_words, w1_scales, w2, gain, wgs, page0, offs2, offs3, offs4, swap, wo, fix, wf_words, wf_scales):
    v = unpack_weight(tab_words, tab_scales, "e4m3")[:, unstriped(offs)]
    w1 = unpack_weight(w1_words, w1_scales, "e2m1")
    wf = unpack_weight(wf_words, wf_scales, "e4m3")
    level = np.tanh(w1.T @ v)
    swing = np.sin(mxq(f64(w2), 0, "e4m3").T @ v)
    h = f64(gain)[:, None] * (level + swing)
    page = f64(page0).copy()
    page[:, unstriped(offs2)] = np.tile(f64(wgs), (H // 128, 1)) * h
    a = page[:, unstriped(offs3)]
    b = page[:, unstriped(offs4)]
    page[:, unstriped(offs3)] = np.maximum(a, b)
    page[:, unstriped(offs4)] = a + f64(swap)[:, None] * b
    pq = mxq(page, 0, "e4m3")
    fq = mxq(f64(fix), 0, "e4m3")
    return mxq(f64(wo), 0, "e4m3").T @ pq + wf.T @ fq

@@ -1,0 +1,343 @@
+import math
+from contextlib import ExitStack
+
+import concourse.mybir as mybir
+
+K, T, H, S, T2, PAIRS, M, N = 1024, 2048, 512, 512, 1024, 256, 512, 512
+FLOPS = 2 * (2 * K * H * S + H * N * T2 + M * N * T2)
+
+F32 = mybir.dt.float32
+BF16 = mybir.dt.bfloat16
+I32 = mybir.dt.int32
+U32 = mybir.dt.uint32
+U16 = mybir.dt.uint16
+U8 = mybir.dt.uint8
+FP8X4 = mybir.dt.float8_e4m3fn_x4
+FP4X4 = mybir.dt.float4_e2m1fn_x4
+ACT = mybir.ActivationFunctionType
+ALU = mybir.AluOpType
+
+P = 128
+PACK = 4
+PASS = P * PACK
+QUADS = 4
+QUARTER = T2 // 4
+TWO_PI = 2.0 * math.pi
+ROUNDER = 1.5 * 2.0**23
+SLOT_ORDER = (2, 0, 1, 3)
+
+
+def tile_list_squad_trade_page_kernel(tc, tab_words, tab_scales, offs, w1_words, w1_scales, w2, gain, wgs,
+                                                page0, offs2, offs3, offs4, swap, wo, fix, wf_words, wf_scales, out):
+    nc = tc.nc
+    with ExitStack() as ctx:
+        keep = ctx.enter_context(tc.tile_pool(name="keep", bufs=1))
+        ring = ctx.enter_context(tc.tile_pool(name="ring", bufs=2))
+        psum = ctx.enter_context(tc.psum_pool(name="psum", bufs=1))
+
+        def held(name, shape, dtype, tag=None):
+            return keep.tile(shape, dtype, name=name, tag=tag or name, align_bytes=64)
+
+        def bank(b, shape, name):
+            return psum.tile(shape, F32, name=name, tag="bank%d" % b)
+
+        def load_scale_rows(plane, scales, engine):
+            passes = scales.shape[0]
+            for q in range(QUADS):
+                engine.dma_start(
+                    out=plane[32 * q : 32 * q + 4, :].rearrange("r (a w) -> r a w", a=passes),
+                    in_=scales[:, 4 * q : 4 * q + 4, :].bitcast(I32).rearrange("a r w -> r a w"),
+                )
+
+        pick = held("pick", [P, S // 16], U16)
+        place = held("place", [P, S // 16], U16)
+        left = held("left", [P, PAIRS // 16], U16)
+        right = held("right", [P, PAIRS // 16], U16)
+        tab_w = [held("tab_w%d" % a, [P, T], I32) for a in range(2)]
+        tab_s = held("tab_s", [P, 2 * T // 4], I32)
+        w1_raw = held("w1_raw", [P, 2 * H // 2], I32)
+        w1_sraw = held("w1_sraw", [P, 2 * H // 4], I32)
+        wf_s = held("wf_s", [P, N // 4], I32)
+        nc.vector.memset(tab_s[:], 0)
+        nc.gpsimd.memset(w1_sraw[:], 0)
+
+        w2_raw0 = held("w2_raw0", [P, PACK, H], F32)
+        w2_raw1 = [held("w2_raw1_%d" % h, [P, PACK, H // 2], F32) for h in range(2)]
+        gain_t = held("gain_t", [P, PACK], F32)
+        swap_t = held("swap_t", [P, PACK], F32)
+        wg_raw = held("wg_raw", [P, PACK * S], F32)
+        page = [held("page%d" % t, [P, T2], F32) for t in range(PACK)]
+        wo_raw = held("wo_raw", [P, PACK, N], F32)
+        fix_raw = [held("fix_raw%d" % h, [P, PACK, T2 // 2], F32) for h in range(2)]
+        wf_w = held("wf_w", [P, N], I32)
+
+        def tab_pass(a):
+            return tab_words[a].rearrange("p t i -> p (t i)").bitcast(I32)
+
+        w2_v = w2.rearrange("(a p j) c -> a p j c", a=2, j=PACK)
+        page_v = page0.rearrange("(p t) c -> t p c", t=PACK)
+        fix_v = fix.rearrange("(p j) c -> p j c", j=PACK)
+
+        nc.sync.dma_start(tab_w[0][:], tab_pass(0))
+        nc.sync.dma_start(pick[:], offs)
+        load_scale_rows(tab_s, tab_scales, nc.sync)
+        nc.sync.dma_start(w1_raw[:].rearrange("p (a w) -> p a w", a=2),
+                          w1_words.bitcast(I32).rearrange("a p w -> p a w"))
+        nc.sync.dma_start(w2_raw0[:], w2_v[0])
+        load_scale_rows(w1_sraw, w1_scales, nc.sync)
+        nc.sync.dma_start(tab_w[1][:], tab_pass(1))
+        for h in range(2):
+            nc.sync.dma_start(w2_raw1[h][:], w2_v[1][:, :, h * (H // 2) : (h + 1) * (H // 2)])
+        nc.sync.dma_start(gain_t[:], gain.rearrange("(p t) -> p t", t=PACK))
+        for q in range(QUADS):
+            nc.sync.dma_start(wg_raw[32 * q : 32 * q + 32, :], wgs.rearrange("(m t) j -> m (t j)", t=PACK))
+        nc.sync.dma_start(place[:], offs2)
+        nc.sync.dma_start(page[SLOT_ORDER[0]][:], page_v[SLOT_ORDER[0]])
+        nc.sync.dma_start(page[SLOT_ORDER[1]][:], page_v[SLOT_ORDER[1]])
+        nc.sync.dma_start(left[:], offs3)
+        nc.sync.dma_start(right[:], offs4)
+        nc.sync.dma_start(swap_t[:], swap.rearrange("(p t) -> p t", t=PACK))
+        nc.sync.dma_start(page[SLOT_ORDER[2]][:], page_v[SLOT_ORDER[2]])
+        nc.sync.dma_start(wo_raw[:], wo.rearrange("(p j) c -> p j c", j=PACK))
+        nc.sync.dma_start(page[SLOT_ORDER[3]][:], page_v[SLOT_ORDER[3]])
+        nc.gpsimd.memset(wf_s[:], 0)
+        load_scale_rows(wf_s, wf_scales, nc.sync)
+        nc.sync.dma_start(wf_w[:], wf_words[0].rearrange("p c i -> p (c i)").bitcast(I32))
+        for h in range(2):
+            nc.sync.dma_start(fix_raw[h][:], fix_v[:, :, h * (T2 // 2) : (h + 1) * (T2 // 2)])
+
+        v_w = [held("v_w%d" % a, [P, S], U32) for a in range(2)]
+        v_s = [held("v_s%d" % a, [P, S], U8) for a in range(2)]
+        w1_w = held("w1_w", [P, 2 * H], U16)
+        w1_s = held("w1_s", [P, 2 * H], U8)
+        w2_b = [held("w2_b%d" % a, [P, PACK * H], BF16) for a in range(2)]
+        w2_w = [held("w2_w%d" % a, [P, H], U32) for a in range(2)]
+        w2_s = [held("w2_s%d" % a, [P, H], U8) for a in range(2)]
+
+        def deal_w2(copy, a, raw, m0, m1):
+            copy(out=w2_b[a][:].rearrange("p (t m j) -> p m j t", t=PACK, j=PACK)[:, m0:m1],
+                 in_=raw[:].rearrange("p j (m t) -> p m j t", t=PACK))
+
+        def quantise(words, scales, grouped):
+            nc.vector.quantize_mx(out=words.bitcast(FP8X4), scales=scales, in_=grouped)
+
+        for a in range(2):
+            nc.vector.tensor_copy(v_s[a][:], tab_s[:].bitcast(U8)[:, a * T : (a + 1) * T].indirect(pick[:]))
+        nc.vector.tensor_copy(v_w[0][:], tab_w[0][:].bitcast(U32).indirect(pick[:]))
+        nc.vector.tensor_copy(out=w1_w[:].rearrange("p (a t m) -> p a m t", a=2, t=PACK),
+                              in_=w1_raw[:].bitcast(U16).rearrange("p (a m t) -> p a m t", a=2, t=PACK))
+        nc.vector.tensor_copy(out=w1_s[:].rearrange("p (a t m) -> p a m t", a=2, t=PACK),
+                              in_=w1_sraw[:].bitcast(U8).rearrange("p (a m t) -> p a m t", a=2, t=PACK))
+        deal_w2(nc.scalar.copy, 0, w2_raw0, 0, P)
+        quantise(w2_w[0][:], w2_s[0][:], w2_b[0][:])
+        nc.vector.tensor_copy(v_w[1][:], tab_w[1][:].bitcast(U32).indirect(pick[:]))
+        deal_w2(nc.vector.tensor_copy, 1, w2_raw1[0], 0, P // 2)
+        deal_w2(nc.vector.tensor_copy, 1, w2_raw1[1], P // 2, P)
+        quantise(w2_w[1][:], w2_s[1][:], w2_b[1][:])
+
+        level_ps = {t: bank(i, [P, S], "level_ps%d" % t) for i, t in enumerate(SLOT_ORDER)}
+        swing_ps = {t: bank(4 + i, [P, S], "swing_ps%d" % t) for i, t in enumerate(SLOT_ORDER)}
+
+        def level_pass(a, t):
+            c0 = a * H + t * P
+            nc.tensor.matmul_mx(out=level_ps[t][:], lhsT=w1_w[:].bitcast(U8)[:, 2 * c0 : 2 * (c0 + P)].bitcast(FP4X4),
+                                lhsT_scale=w1_s[:, c0 : c0 + P], rhs=v_w[a][:].bitcast(FP8X4), rhs_scale=v_s[a][:],
+                                start=(a == 0), stop=(a == 1))
+
+        def swing_pass(a, t):
+            cols = slice(t * P, (t + 1) * P)
+            nc.tensor.matmul_mx(out=swing_ps[t][:], lhsT=w2_w[a][:, cols].bitcast(FP8X4), lhsT_scale=w2_s[a][:, cols],
+                                rhs=v_w[a][:].bitcast(FP8X4), rhs_scale=v_s[a][:], start=(a == 0), stop=(a == 1))
+
+        for a in range(2):
+            for t in SLOT_ORDER:
+                level_pass(a, t)
+            for t in SLOT_ORDER:
+                swing_pass(a, t)
+
+        level = {t: held("level%d" % t, [P, S], F32) for t in SLOT_ORDER}
+        for t in SLOT_ORDER:
+            nc.scalar.activation(level[t][:], level_ps[t][:], ACT.Tanh)
+
+        s0, s1, s2, s3 = SLOT_ORDER
+        turns, angle, form = {}, {}, {}
+        page_b = [held("page_b%d" % q, [P, QUARTER * PACK], BF16) for q in range(4)]
+        fix_w = {}
+        swing = {t: held("swing%d" % t, [P, S], F32)[:] for t in SLOT_ORDER}
+        weight = {t: held("weight%d" % t, [P, S], F32)[:] for t in SLOT_ORDER}
+        a_t = {s0: level[s3][:, 0:PAIRS], s1: level[s3][:, PAIRS:S], s2: level[s3][:, 0:PAIRS], s3: level[s3][:, PAIRS:S]}
+        b_t = {s0: swing[s3][:, 0:PAIRS], s1: weight[s3][:, 0:PAIRS], s2: swing[s3][:, 0:PAIRS], s3: weight[s3][:, 0:PAIRS]}
+        top = {t: held("top%d" % t, [P, PAIRS], F32)[:] for t in (s1, s2, s3)}
+        top[s0] = wo_raw[:, 0, 0:PAIRS]
+        scaled_b = {t: held("scaled_b%d" % t, [P, PAIRS], F32)[:] for t in (s3,)}
+        scaled_b[s0] = fix_raw[0][:, 0, 0:PAIRS]
+        scaled_b[s1] = fix_raw[1][:, 0, 0:PAIRS]
+
+        def count_turns(t, j0=0, j1=S):
+            shifted = ring.tile([P, j1 - j0], U32, name="shifted")
+            nc.scalar.activation(shifted[:], swing_ps[t][:, j0:j1], ACT.Copy, bias=ROUNDER, scale=1.0 / TWO_PI)
+            turns[t, j0] = ring.tile([P, j1 - j0], F32, name="turns")
+            nc.scalar.activation(turns[t, j0][:], shifted[:], ACT.Copy, bias=-ROUNDER, scale=1.0)
+
+        def reduce_angle(t, j0=0, j1=S):
+            angle[t, j0] = ring.tile([P, j1 - j0], F32, name="angle")
+            nc.vector.scalar_tensor_tensor(angle[t, j0][:], turns[t, j0][:], -TWO_PI, swing_ps[t][:, j0:j1],
+                                           ALU.mult, ALU.add)
+
+        def sine(t, j0=0, j1=S):
+            nc.scalar.activation(swing[t][:, j0:j1], angle[t, j0][:], ACT.Sin)
+
+        def weigh(t):
+            nc.scalar.activation(weight[t], wg_raw[:, t * S : (t + 1) * S], ACT.Copy, scale=gain_t[:, t : t + 1])
+
+        def add_parts(t, j0=0, j1=S):
+            form[t, j0] = ring.tile([P, j1 - j0], F32, name="form")
+            nc.vector.tensor_tensor(form[t, j0][:], level[t][:, j0:j1], swing[t][:, j0:j1], ALU.add)
+
+        def put_form(t, j0=0, j1=S):
+            nc.vector.tensor_tensor(page[t][:].indirect(place[:, j0 // 16 : j1 // 16]), form[t, j0][:],
+                                    weight[t][:, j0:j1], ALU.mult)
+
+        def fetch_left(t):
+            nc.vector.tensor_copy(a_t[t], page[t][:].indirect(left[:]))
+
+        def fetch_right(t):
+            nc.vector.tensor_copy(b_t[t], page[t][:].indirect(right[:]))
+            if t == s2:
+                scaled_b[t] = held("scaled_b%d" % t, [P, PAIRS], F32, tag="page%d" % s0)[:]
+            nc.scalar.activation(scaled_b[t], b_t[t], ACT.Copy, scale=swap_t[:, t : t + 1])
+
+        def larger(t):
+            nc.vector.tensor_tensor(top[t], a_t[t], b_t[t], ALU.max)
+
+        def put_left(t):
+            nc.vector.tensor_copy(page[t][:].indirect(left[:]), top[t])
+
+        def put_right(t):
+            nc.vector.tensor_tensor(page[t][:].indirect(right[:]), a_t[t], scaled_b[t], ALU.add)
+
+
+        def weave_page(copy, t, q):
+            copy(out=page_b[q][:].rearrange("p (c j) -> p c j", j=PACK)[:, :, t], in_=page[t][:, q * QUARTER : (q + 1) * QUARTER])
+
+        def weave(grouped, raw):
+            nc.scalar.copy(out=grouped[:].rearrange("p (c i j) -> p c j i", i=4, j=PACK),
+                           in_=raw[:].rearrange("p j (c i) -> p c j i", i=4))
+
+        wo_b = held("wo_b", [P, PACK * N], BF16)
+        wo_w = held("wo_w", [P, N], U32)
+        wo_s = held("wo_s", [P, N], U8)
+        fix_b = [held("fix_b%d" % h, [P, PACK * T2 // 2], BF16) for h in range(2)]
+        fix_s = [held("fix_s%d" % h, [P, T2 // 2], U8) for h in range(2)]
+        page_w = [held("page_w%d" % q, [P, QUARTER], U32) for q in range(4)]
+        page_s = [held("page_s%d" % q, [P, QUARTER], U8) for q in range(4)]
+        score_ps = {}
+
+        def fixture_passes(h):
+            for q in (2 * h, 2 * h + 1):
+                cols = slice((q % 2) * QUARTER, (q % 2 + 1) * QUARTER)
+                for pair in range(2):
+                    score_ps[q, pair] = bank(2 * q + pair, [P, 2, QUARTER], "score_ps%d_%d" % (q, pair))
+                    for i in range(2):
+                        n0 = (2 * pair + i) * P
+                        nc.tensor.matmul_mx(out=score_ps[q, pair][:, i, :], lhsT=wf_w[:, n0 : n0 + P].bitcast(FP8X4),
+                                            lhsT_scale=wf_s[:].bitcast(U8)[:, n0 : n0 + P],
+                                            rhs=fix_w[h][:, cols].bitcast(FP8X4), rhs_scale=fix_s[h][:, cols],
+                                            start=(i == 0), stop=False)
+
+        out_v = out.rearrange("(n p) c -> p n c", p=P)
+
+        def page_passes(q):
+            for pair in range(2):
+                for i in range(2):
+                    n0 = (2 * pair + i) * P
+                    nc.tensor.matmul_mx(out=score_ps[q, pair][:, i, :], lhsT=wo_w[:, n0 : n0 + P].bitcast(FP8X4),
+                                        lhsT_scale=wo_s[:, n0 : n0 + P], rhs=page_w[q][:].bitcast(FP8X4),
+                                        rhs_scale=page_s[q][:], start=False, stop=(i == 1))
+
+        def store(copy, q, pair):
+            score = held("score%d_%d" % (q, pair), [P, 2, QUARTER], F32)
+            copy(out=score[:], in_=score_ps[q, pair][:])
+            nc.sync.dma_start(out_v[:, 2 * pair : 2 * pair + 2, q * QUARTER : (q + 1) * QUARTER], score[:])
+
+        def quantise_fixtures(h, tag):
+            fix_w[h] = held("fix_w%d" % h, [P, T2 // 2], U32, tag=tag)
+            quantise(fix_w[h][:], fix_s[h][:], fix_b[h][:])
+            fixture_passes(h)
+
+        half = S // 2
+        count_turns(s0, 0, half)
+        count_turns(s0, half, S)
+        reduce_angle(s0, 0, half)
+        reduce_angle(s0, half, S)
+        sine(s0, 0, half)
+        sine(s0, half, S)
+        nc.vector.tensor_scalar(weight[s0], wg_raw[:, s0 * S : (s0 + 1) * S], gain_t[:, s0 : s0 + 1], None, ALU.mult)
+        add_parts(s0, 0, half)
+        add_parts(s0, half, S)
+        count_turns(s1)
+        put_form(s0, 0, half)
+        reduce_angle(s1)
+        sine(s1)
+        put_form(s0, half, S)
+        count_turns(s2)
+        weigh(s1)
+        add_parts(s1)
+        reduce_angle(s2)
+        count_turns(s3)
+        sine(s2)
+        weigh(s2)
+        put_form(s1)
+        add_parts(s2)
+        reduce_angle(s3)
+        sine(s3)
+        weigh(s3)
+        put_form(s2)
+        weave(wo_b, wo_raw)
+        weave(fix_b[0], fix_raw[0])
+        weave(fix_b[1], fix_raw[1])
+        add_parts(s3)
+        fetch_left(s0)
+        fetch_right(s0)
+        put_form(s3)
+        fetch_left(s1)
+        larger(s0)
+        fetch_right(s1)
+        put_left(s0)
+        larger(s1)
+        quantise(wo_w[:], wo_s[:], wo_b[:])
+        put_right(s0)
+        for q in range(4):
+            weave_page(nc.scalar.copy, s0, q)
+        put_right(s1)
+        fetch_left(s2)
+        put_left(s1)
+        fetch_right(s2)
+        fetch_left(s3)
+        larger(s2)
+        fetch_right(s3)
+        put_left(s2)
+        larger(s3)
+        for q in range(4):
+            weave_page(nc.scalar.copy, s1, q)
+        put_right(s2)
+        for q in range(4):
+            weave_page(nc.scalar.copy, s2, q)
+        quantise_fixtures(0, "top%d" % s2)
+        put_left(s3)
+        quantise_fixtures(1, "page%d" % s0)
+        put_right(s3)
+
+        def quantise_page(q):
+            quantise(page_w[q][:], page_s[q][:], page_b[q][:])
+            page_passes(q)
+
+        weave_page(nc.vector.tensor_copy, s3, 0)
+        weave_page(nc.scalar.copy, s3, 1)
+        weave_page(nc.vector.tensor_copy, s3, 2)
+        weave_page(nc.scalar.copy, s3, 3)
+        for q in (0, 2, 1, 3):
+            quantise_page(q)
+        for q in (0, 2, 1, 3):
+            store(nc.scalar.copy, q, 0)
+            store(nc.vector.tensor_copy, q, 1)

@@ -58,11 +58,15 @@ def tile_list_squad_trade_page_kernel(tc, tab_words, tab_scales, offs, w1_words,
         w1_raw = held("w1_raw", [P, 2 * H // 2], I32)
         w1_sraw = held("w1_sraw", [P, 2 * H // 4], I32)
         wf_s = held("wf_s", [P, N // 4], I32)
-        nc.vector.memset(tab_s[:], 0)
+        nc.vector.memset(tab_s[:, 0 : 3 * T // 8], 0)
+        nc.gpsimd.memset(tab_s[:, 3 * T // 8 : T // 2], 0)
+        warm_in = held("warm_in", [P, 1], F32)
+        warm_out = held("warm_out", [P, 1], F32)
+        nc.gpsimd.memset(warm_in[:], 0.0)
+        nc.scalar.activation(warm_out[:], warm_in[:], ACT.Silu)
         nc.gpsimd.memset(w1_sraw[:], 0)
 
-        w2_raw0 = held("w2_raw0", [P, PACK, H], F32)
-        w2_raw1 = [held("w2_raw1_%d" % h, [P, PACK, H // 2], F32) for h in range(2)]
+        w2_raw = [held("w2_raw%d" % a, [P, PACK, H], F32) for a in range(2)]
         gain_t = held("gain_t", [P, PACK], F32)
         swap_t = held("swap_t", [P, PACK], F32)
         wg_raw = held("wg_raw", [P, PACK * S], F32)
@@ -78,16 +82,15 @@ def tile_list_squad_trade_page_kernel(tc, tab_words, tab_scales, offs, w1_words,
         page_v = page0.rearrange("(p t) c -> t p c", t=PACK)
         fix_v = fix.rearrange("(p j) c -> p j c", j=PACK)
 
-        nc.sync.dma_start(tab_w[0][:], tab_pass(0))
+        nc.sync.dma_start(w2_raw[0][:], w2_v[0])
         nc.sync.dma_start(pick[:], offs)
         load_scale_rows(tab_s, tab_scales, nc.sync)
+        nc.sync.dma_start(w2_raw[1][:], w2_v[1])
+        nc.sync.dma_start(tab_w[0][:], tab_pass(0))
         nc.sync.dma_start(w1_raw[:].rearrange("p (a w) -> p a w", a=2),
                           w1_words.bitcast(I32).rearrange("a p w -> p a w"))
-        nc.sync.dma_start(w2_raw0[:], w2_v[0])
         load_scale_rows(w1_sraw, w1_scales, nc.sync)
         nc.sync.dma_start(tab_w[1][:], tab_pass(1))
-        for h in range(2):
-            nc.sync.dma_start(w2_raw1[h][:], w2_v[1][:, :, h * (H // 2) : (h + 1) * (H // 2)])
         nc.sync.dma_start(gain_t[:], gain.rearrange("(p t) -> p t", t=PACK))
         for q in range(QUADS):
             nc.sync.dma_start(wg_raw[32 * q : 32 * q + 32, :], wgs.rearrange("(m t) j -> m (t j)", t=PACK))
@@ -98,8 +101,8 @@ def tile_list_squad_trade_page_kernel(tc, tab_words, tab_scales, offs, w1_words,
         nc.sync.dma_start(right[:], offs4)
         nc.sync.dma_start(swap_t[:], swap.rearrange("(p t) -> p t", t=PACK))
         nc.sync.dma_start(page[SLOT_ORDER[2]][:], page_v[SLOT_ORDER[2]])
-        nc.sync.dma_start(wo_raw[:], wo.rearrange("(p j) c -> p j c", j=PACK))
         nc.sync.dma_start(page[SLOT_ORDER[3]][:], page_v[SLOT_ORDER[3]])
+        nc.sync.dma_start(wo_raw[:], wo.rearrange("(p j) c -> p j c", j=PACK))
         nc.gpsimd.memset(wf_s[:], 0)
         load_scale_rows(wf_s, wf_scales, nc.sync)
         nc.sync.dma_start(wf_w[:], wf_words[0].rearrange("p c i -> p (c i)").bitcast(I32))
@@ -114,53 +117,60 @@ def tile_list_squad_trade_page_kernel(tc, tab_words, tab_scales, offs, w1_words,
         w2_w = [held("w2_w%d" % a, [P, H], U32) for a in range(2)]
         w2_s = [held("w2_s%d" % a, [P, H], U8) for a in range(2)]
 
-        def deal_w2(copy, a, raw, m0, m1):
-            copy(out=w2_b[a][:].rearrange("p (t m j) -> p m j t", t=PACK, j=PACK)[:, m0:m1],
-                 in_=raw[:].rearrange("p j (m t) -> p m j t", t=PACK))
+        def deal_w2(copy, a):
+            copy(out=w2_b[a][:].rearrange("p (t m j) -> p m j t", t=PACK, j=PACK),
+                 in_=w2_raw[a][:].rearrange("p j (m t) -> p m j t", t=PACK))
 
         def quantise(words, scales, grouped):
             nc.vector.quantize_mx(out=words.bitcast(FP8X4), scales=scales, in_=grouped)
 
+        half = S // 2
         for a in range(2):
             nc.vector.tensor_copy(v_s[a][:], tab_s[:].bitcast(U8)[:, a * T : (a + 1) * T].indirect(pick[:]))
-        nc.vector.tensor_copy(v_w[0][:], tab_w[0][:].bitcast(U32).indirect(pick[:]))
-        nc.vector.tensor_copy(out=w1_w[:].rearrange("p (a t m) -> p a m t", a=2, t=PACK),
-                              in_=w1_raw[:].bitcast(U16).rearrange("p (a m t) -> p a m t", a=2, t=PACK))
-        nc.vector.tensor_copy(out=w1_s[:].rearrange("p (a t m) -> p a m t", a=2, t=PACK),
-                              in_=w1_sraw[:].bitcast(U8).rearrange("p (a m t) -> p a m t", a=2, t=PACK))
-        deal_w2(nc.scalar.copy, 0, w2_raw0, 0, P)
-        quantise(w2_w[0][:], w2_s[0][:], w2_b[0][:])
-        nc.vector.tensor_copy(v_w[1][:], tab_w[1][:].bitcast(U32).indirect(pick[:]))
-        deal_w2(nc.vector.tensor_copy, 1, w2_raw1[0], 0, P // 2)
-        deal_w2(nc.vector.tensor_copy, 1, w2_raw1[1], P // 2, P)
-        quantise(w2_w[1][:], w2_s[1][:], w2_b[1][:])
-
-        level_ps = {t: bank(i, [P, S], "level_ps%d" % t) for i, t in enumerate(SLOT_ORDER)}
-        swing_ps = {t: bank(4 + i, [P, S], "swing_ps%d" % t) for i, t in enumerate(SLOT_ORDER)}
-
-        def level_pass(a, t):
-            c0 = a * H + t * P
-            nc.tensor.matmul_mx(out=level_ps[t][:], lhsT=w1_w[:].bitcast(U8)[:, 2 * c0 : 2 * (c0 + P)].bitcast(FP4X4),
-                                lhsT_scale=w1_s[:, c0 : c0 + P], rhs=v_w[a][:].bitcast(FP8X4), rhs_scale=v_s[a][:],
-                                start=(a == 0), stop=(a == 1))
-
-        def swing_pass(a, t):
-            cols = slice(t * P, (t + 1) * P)
-            nc.tensor.matmul_mx(out=swing_ps[t][:], lhsT=w2_w[a][:, cols].bitcast(FP8X4), lhsT_scale=w2_s[a][:, cols],
-                                rhs=v_w[a][:].bitcast(FP8X4), rhs_scale=v_s[a][:], start=(a == 0), stop=(a == 1))
-
         for a in range(2):
-            for t in SLOT_ORDER:
-                level_pass(a, t)
-            for t in SLOT_ORDER:
-                swing_pass(a, t)
-
-        level = {t: held("level%d" % t, [P, S], F32) for t in SLOT_ORDER}
-        for t in SLOT_ORDER:
-            nc.scalar.activation(level[t][:], level_ps[t][:], ACT.Tanh)
+            deal_w2(nc.scalar.copy, a)
+        quantise(w2_w[0][:], w2_s[0][:], w2_b[0][:])
+        nc.vector.tensor_copy(out=w1_w[:].rearrange("p (a t m) -> p a t m", a=2, t=PACK),
+                              in_=w1_raw[:].bitcast(U16).rearrange("p (a m t) -> p a t m", a=2, t=PACK))
+        nc.vector.tensor_copy(out=w1_s[:].rearrange("p (a t m) -> p a t m", a=2, t=PACK),
+                              in_=w1_sraw[:].bitcast(U8).rearrange("p (a m t) -> p a t m", a=2, t=PACK))
+        quantise(w2_w[1][:], w2_s[1][:], w2_b[1][:])
+        nc.vector.tensor_copy(v_w[0][:], tab_w[0][:].bitcast(U32).indirect(pick[:]))
+        for j0 in (0, half):
+            nc.vector.tensor_copy(v_w[1][:, j0 : j0 + half],
+                                  tab_w[1][:].bitcast(U32).indirect(pick[:, j0 // 16 : (j0 + half) // 16]))
 
         s0, s1, s2, s3 = SLOT_ORDER
-        turns, angle, form = {}, {}, {}
+        level_ps, swing_ps = {}, {}
+
+        def first_products(b, t, j0=0, j1=S):
+            level_ps[t, j0] = bank(b, [P, j1 - j0], "level_ps%d_%d" % (t, j0))
+            swing_ps[t, j0] = bank(4 + b, [P, j1 - j0], "swing_ps%d_%d" % (t, j0))
+            cols = slice(t * P, (t + 1) * P)
+            for a in range(2):
+                picked = dict(rhs=v_w[a][:, j0:j1].bitcast(FP8X4), rhs_scale=v_s[a][:, j0:j1],
+                              start=(a == 0), stop=(a == 1))
+                nc.tensor.matmul_mx(out=swing_ps[t, j0][:], lhsT=w2_w[a][:, cols].bitcast(FP8X4),
+                                    lhsT_scale=w2_s[a][:, cols], **picked)
+                c0 = a * H + t * P
+                nc.tensor.matmul_mx(out=level_ps[t, j0][:],
+                                    lhsT=w1_w[:].bitcast(U8)[:, 2 * c0 : 2 * (c0 + P)].bitcast(FP4X4),
+                                    lhsT_scale=w1_s[:, c0 : c0 + P], **picked)
+
+        first_products(0, s0, 0, half)
+        first_products(3, s0, half, S)
+        first_products(1, s1)
+        first_products(2, s2)
+
+        level = {t: held("level%d" % t, [P, S], F32) for t in SLOT_ORDER}
+
+        def squash(t, j0=0, j1=S):
+            nc.scalar.activation(level[t][:, j0:j1], level_ps[t, j0][:], ACT.Tanh)
+
+        turns = {t: held("turns%d" % t, [P, S], F32) for t in SLOT_ORDER}
+        angle = {}
+        form = {(s0, 0): held("form_first", [P, half], F32)[:], (s0, half): turns[s1][:, 0:half],
+                (s1, 0): turns[s2][:], (s2, 0): turns[s3][:], (s3, 0): held("form_last", [P, S], F32)[:]}
         page_b = [held("page_b%d" % q, [P, QUARTER * PACK], BF16) for q in range(4)]
         fix_w = {}
         swing = {t: held("swing%d" % t, [P, S], F32)[:] for t in SLOT_ORDER}
@@ -175,13 +185,12 @@ def tile_list_squad_trade_page_kernel(tc, tab_words, tab_scales, offs, w1_words,
 
         def count_turns(t, j0=0, j1=S):
             shifted = ring.tile([P, j1 - j0], U32, name="shifted")
-            nc.scalar.activation(shifted[:], swing_ps[t][:, j0:j1], ACT.Copy, bias=ROUNDER, scale=1.0 / TWO_PI)
-            turns[t, j0] = ring.tile([P, j1 - j0], F32, name="turns")
-            nc.scalar.activation(turns[t, j0][:], shifted[:], ACT.Copy, bias=-ROUNDER, scale=1.0)
+            nc.scalar.activation(shifted[:], swing_ps[t, j0][:], ACT.Copy, bias=ROUNDER, scale=1.0 / TWO_PI)
+            nc.scalar.activation(turns[t][:, j0:j1], shifted[:], ACT.Copy, bias=-ROUNDER, scale=1.0)
 
         def reduce_angle(t, j0=0, j1=S):
             angle[t, j0] = ring.tile([P, j1 - j0], F32, name="angle")
-            nc.vector.scalar_tensor_tensor(angle[t, j0][:], turns[t, j0][:], -TWO_PI, swing_ps[t][:, j0:j1],
+            nc.vector.scalar_tensor_tensor(angle[t, j0][:], turns[t][:, j0:j1], -TWO_PI, swing_ps[t, j0][:],
                                            ALU.mult, ALU.add)
 
         def sine(t, j0=0, j1=S):
@@ -191,11 +200,10 @@ def tile_list_squad_trade_page_kernel(tc, tab_words, tab_scales, offs, w1_words,
             nc.scalar.activation(weight[t], wg_raw[:, t * S : (t + 1) * S], ACT.Copy, scale=gain_t[:, t : t + 1])
 
         def add_parts(t, j0=0, j1=S):
-            form[t, j0] = ring.tile([P, j1 - j0], F32, name="form")
-            nc.vector.tensor_tensor(form[t, j0][:], level[t][:, j0:j1], swing[t][:, j0:j1], ALU.add)
+            nc.vector.tensor_tensor(form[t, j0], level[t][:, j0:j1], swing[t][:, j0:j1], ALU.add)
 
         def put_form(t, j0=0, j1=S):
-            nc.vector.tensor_tensor(page[t][:].indirect(place[:, j0 // 16 : j1 // 16]), form[t, j0][:],
+            nc.vector.tensor_tensor(page[t][:].indirect(place[:, j0 // 16 : j1 // 16]), form[t, j0],
                                     weight[t][:, j0:j1], ALU.mult)
 
         def fetch_left(t):
@@ -265,34 +273,33 @@ def tile_list_squad_trade_page_kernel(tc, tab_words, tab_scales, offs, w1_words,
             quantise(fix_w[h][:], fix_s[h][:], fix_b[h][:])
             fixture_passes(h)
 
-        half = S // 2
         count_turns(s0, 0, half)
-        count_turns(s0, half, S)
+        squash(s0, 0, half)
         reduce_angle(s0, 0, half)
-        reduce_angle(s0, half, S)
+        count_turns(s0, half, S)
         sine(s0, 0, half)
-        sine(s0, half, S)
+        squash(s0, half, S)
+        first_products(0, s3)
+        reduce_angle(s0, half, S)
         nc.vector.tensor_scalar(weight[s0], wg_raw[:, s0 * S : (s0 + 1) * S], gain_t[:, s0 : s0 + 1], None, ALU.mult)
         add_parts(s0, 0, half)
-        add_parts(s0, half, S)
         count_turns(s1)
+        sine(s0, half, S)
         put_form(s0, 0, half)
         reduce_angle(s1)
-        sine(s1)
+        add_parts(s0, half, S)
         put_form(s0, half, S)
-        count_turns(s2)
-        weigh(s1)
-        add_parts(s1)
-        reduce_angle(s2)
-        count_turns(s3)
-        sine(s2)
-        weigh(s2)
-        put_form(s1)
-        add_parts(s2)
-        reduce_angle(s3)
+        for t, after in ((s1, s2), (s2, s3)):
+            sine(t)
+            count_turns(after)
+            squash(t)
+            weigh(t)
+            reduce_angle(after)
+            add_parts(t)
+            put_form(t)
         sine(s3)
+        squash(s3)
         weigh(s3)
-        put_form(s2)
         weave(wo_b, wo_raw)
         weave(fix_b[0], fix_raw[0])
         weave(fix_b[1], fix_raw[1])
@@ -340,4 +347,4 @@ def tile_list_squad_trade_page_kernel(tc, tab_words, tab_scales, offs, w1_words,
             quantise_page(q)
         for q in (0, 2, 1, 3):
             store(nc.scalar.copy, q, 0)
-            store(nc.vector.tensor_copy, q, 1)
+            store(nc.scalar.copy if q == 0 else nc.vector.tensor_copy, q, 1)

import math
from contextlib import ExitStack

import concourse.mybir as mybir

K, T, H, S, T2, PAIRS, M, N = 1024, 2048, 512, 512, 1024, 256, 512, 512
FLOPS = 2 * (2 * K * H * S + H * N * T2 + M * N * T2)

F32 = mybir.dt.float32
BF16 = mybir.dt.bfloat16
I32 = mybir.dt.int32
U32 = mybir.dt.uint32
U16 = mybir.dt.uint16
U8 = mybir.dt.uint8
FP8X4 = mybir.dt.float8_e4m3fn_x4
FP4X4 = mybir.dt.float4_e2m1fn_x4
ACT = mybir.ActivationFunctionType
ALU = mybir.AluOpType

P = 128
PACK = 4
PASS = P * PACK
QUADS = 4
QUARTER = T2 // 4
TWO_PI = 2.0 * math.pi
ROUNDER = 1.5 * 2.0**23
SLOT_ORDER = (2, 0, 1, 3)


def tile_list_squad_trade_page_kernel(tc, tab_words, tab_scales, offs, w1_words, w1_scales, w2, gain, wgs,
                                                page0, offs2, offs3, offs4, swap, wo, fix, wf_words, wf_scales, out):
    nc = tc.nc
    with ExitStack() as ctx:
        keep = ctx.enter_context(tc.tile_pool(name="keep", bufs=1))
        ring = ctx.enter_context(tc.tile_pool(name="ring", bufs=2))
        psum = ctx.enter_context(tc.psum_pool(name="psum", bufs=1))

        def held(name, shape, dtype, tag=None):
            return keep.tile(shape, dtype, name=name, tag=tag or name, align_bytes=64)

        def bank(b, shape, name):
            return psum.tile(shape, F32, name=name, tag="bank%d" % b)

        def load_scale_rows(plane, scales, engine):
            passes = scales.shape[0]
            for q in range(QUADS):
                engine.dma_start(
                    out=plane[32 * q : 32 * q + 4, :].rearrange("r (a w) -> r a w", a=passes),
                    in_=scales[:, 4 * q : 4 * q + 4, :].bitcast(I32).rearrange("a r w -> r a w"),
                )

        pick = held("pick", [P, S // 16], U16)
        place = held("place", [P, S // 16], U16)
        left = held("left", [P, PAIRS // 16], U16)
        right = held("right", [P, PAIRS // 16], U16)
        tab_w = [held("tab_w%d" % a, [P, T], I32) for a in range(2)]
        tab_s = held("tab_s", [P, 2 * T // 4], I32)
        w1_raw = held("w1_raw", [P, 2 * H // 2], I32)
        w1_sraw = held("w1_sraw", [P, 2 * H // 4], I32)
        wf_s = held("wf_s", [P, N // 4], I32)
        nc.vector.memset(tab_s[:, 0 : 3 * T // 8], 0)
        nc.gpsimd.memset(tab_s[:, 3 * T // 8 : T // 2], 0)
        warm_in = held("warm_in", [P, 1], F32)
        warm_out = held("warm_out", [P, 1], F32)
        nc.gpsimd.memset(warm_in[:], 0.0)
        nc.scalar.activation(warm_out[:], warm_in[:], ACT.Silu)
        nc.gpsimd.memset(w1_sraw[:], 0)

        w2_raw = [held("w2_raw%d" % a, [P, PACK, H], F32) for a in range(2)]
        gain_t = held("gain_t", [P, PACK], F32)
        swap_t = held("swap_t", [P, PACK], F32)
        wg_raw = held("wg_raw", [P, PACK * S], F32)
        page = [held("page%d" % t, [P, T2], F32) for t in range(PACK)]
        wo_raw = held("wo_raw", [P, PACK, N], F32)
        fix_raw = [held("fix_raw%d" % h, [P, PACK, T2 // 2], F32) for h in range(2)]
        wf_w = held("wf_w", [P, N], I32)

        def tab_pass(a):
            return tab_words[a].rearrange("p t i -> p (t i)").bitcast(I32)

        w2_v = w2.rearrange("(a p j) c -> a p j c", a=2, j=PACK)
        page_v = page0.rearrange("(p t) c -> t p c", t=PACK)
        fix_v = fix.rearrange("(p j) c -> p j c", j=PACK)

        nc.sync.dma_start(w2_raw[0][:], w2_v[0])
        nc.sync.dma_start(pick[:], offs)
        load_scale_rows(tab_s, tab_scales, nc.sync)
        nc.sync.dma_start(w2_raw[1][:], w2_v[1])
        nc.sync.dma_start(tab_w[0][:], tab_pass(0))
        nc.sync.dma_start(w1_raw[:].rearrange("p (a w) -> p a w", a=2),
                          w1_words.bitcast(I32).rearrange("a p w -> p a w"))
        load_scale_rows(w1_sraw, w1_scales, nc.sync)
        nc.sync.dma_start(tab_w[1][:], tab_pass(1))
        nc.sync.dma_start(gain_t[:], gain.rearrange("(p t) -> p t", t=PACK))
        for q in range(QUADS):
            nc.sync.dma_start(wg_raw[32 * q : 32 * q + 32, :], wgs.rearrange("(m t) j -> m (t j)", t=PACK))
        nc.sync.dma_start(place[:], offs2)
        nc.sync.dma_start(page[SLOT_ORDER[0]][:], page_v[SLOT_ORDER[0]])
        nc.sync.dma_start(page[SLOT_ORDER[1]][:], page_v[SLOT_ORDER[1]])
        nc.sync.dma_start(left[:], offs3)
        nc.sync.dma_start(right[:], offs4)
        nc.sync.dma_start(swap_t[:], swap.rearrange("(p t) -> p t", t=PACK))
        nc.sync.dma_start(page[SLOT_ORDER[2]][:], page_v[SLOT_ORDER[2]])
        nc.sync.dma_start(page[SLOT_ORDER[3]][:], page_v[SLOT_ORDER[3]])
        nc.sync.dma_start(wo_raw[:], wo.rearrange("(p j) c -> p j c", j=PACK))
        nc.gpsimd.memset(wf_s[:], 0)
        load_scale_rows(wf_s, wf_scales, nc.sync)
        nc.sync.dma_start(wf_w[:], wf_words[0].rearrange("p c i -> p (c i)").bitcast(I32))
        for h in range(2):
            nc.sync.dma_start(fix_raw[h][:], fix_v[:, :, h * (T2 // 2) : (h + 1) * (T2 // 2)])

        v_w = [held("v_w%d" % a, [P, S], U32) for a in range(2)]
        v_s = [held("v_s%d" % a, [P, S], U8) for a in range(2)]
        w1_w = held("w1_w", [P, 2 * H], U16)
        w1_s = held("w1_s", [P, 2 * H], U8)
        w2_b = [held("w2_b%d" % a, [P, PACK * H], BF16) for a in range(2)]
        w2_w = [held("w2_w%d" % a, [P, H], U32) for a in range(2)]
        w2_s = [held("w2_s%d" % a, [P, H], U8) for a in range(2)]

        def deal_w2(copy, a):
            copy(out=w2_b[a][:].rearrange("p (t m j) -> p m j t", t=PACK, j=PACK),
                 in_=w2_raw[a][:].rearrange("p j (m t) -> p m j t", t=PACK))

        def quantise(words, scales, grouped):
            nc.vector.quantize_mx(out=words.bitcast(FP8X4), scales=scales, in_=grouped)

        half = S // 2
        for a in range(2):
            nc.vector.tensor_copy(v_s[a][:], tab_s[:].bitcast(U8)[:, a * T : (a + 1) * T].indirect(pick[:]))
        for a in range(2):
            deal_w2(nc.scalar.copy, a)
        quantise(w2_w[0][:], w2_s[0][:], w2_b[0][:])
        nc.vector.tensor_copy(out=w1_w[:].rearrange("p (a t m) -> p a t m", a=2, t=PACK),
                              in_=w1_raw[:].bitcast(U16).rearrange("p (a m t) -> p a t m", a=2, t=PACK))
        nc.vector.tensor_copy(out=w1_s[:].rearrange("p (a t m) -> p a t m", a=2, t=PACK),
                              in_=w1_sraw[:].bitcast(U8).rearrange("p (a m t) -> p a t m", a=2, t=PACK))
        quantise(w2_w[1][:], w2_s[1][:], w2_b[1][:])
        nc.vector.tensor_copy(v_w[0][:], tab_w[0][:].bitcast(U32).indirect(pick[:]))
        for j0 in (0, half):
            nc.vector.tensor_copy(v_w[1][:, j0 : j0 + half],
                                  tab_w[1][:].bitcast(U32).indirect(pick[:, j0 // 16 : (j0 + half) // 16]))

        s0, s1, s2, s3 = SLOT_ORDER
        level_ps, swing_ps = {}, {}

        def first_products(b, t, j0=0, j1=S):
            level_ps[t, j0] = bank(b, [P, j1 - j0], "level_ps%d_%d" % (t, j0))
            swing_ps[t, j0] = bank(4 + b, [P, j1 - j0], "swing_ps%d_%d" % (t, j0))
            cols = slice(t * P, (t + 1) * P)
            for a in range(2):
                picked = dict(rhs=v_w[a][:, j0:j1].bitcast(FP8X4), rhs_scale=v_s[a][:, j0:j1],
                              start=(a == 0), stop=(a == 1))
                nc.tensor.matmul_mx(out=swing_ps[t, j0][:], lhsT=w2_w[a][:, cols].bitcast(FP8X4),
                                    lhsT_scale=w2_s[a][:, cols], **picked)
                c0 = a * H + t * P
                nc.tensor.matmul_mx(out=level_ps[t, j0][:],
                                    lhsT=w1_w[:].bitcast(U8)[:, 2 * c0 : 2 * (c0 + P)].bitcast(FP4X4),
                                    lhsT_scale=w1_s[:, c0 : c0 + P], **picked)

        first_products(0, s0, 0, half)
        first_products(3, s0, half, S)
        first_products(1, s1)
        first_products(2, s2)

        level = {t: held("level%d" % t, [P, S], F32) for t in SLOT_ORDER}

        def squash(t, j0=0, j1=S):
            nc.scalar.activation(level[t][:, j0:j1], level_ps[t, j0][:], ACT.Tanh)

        turns = {t: held("turns%d" % t, [P, S], F32) for t in SLOT_ORDER}
        angle = {}
        form = {(s0, 0): held("form_first", [P, half], F32)[:], (s0, half): turns[s1][:, 0:half],
                (s1, 0): turns[s2][:], (s2, 0): turns[s3][:], (s3, 0): held("form_last", [P, S], F32)[:]}
        page_b = [held("page_b%d" % q, [P, QUARTER * PACK], BF16) for q in range(4)]
        fix_w = {}
        swing = {t: held("swing%d" % t, [P, S], F32)[:] for t in SLOT_ORDER}
        weight = {t: held("weight%d" % t, [P, S], F32)[:] for t in SLOT_ORDER}
        a_t = {s0: level[s3][:, 0:PAIRS], s1: level[s3][:, PAIRS:S], s2: level[s3][:, 0:PAIRS], s3: level[s3][:, PAIRS:S]}
        b_t = {s0: swing[s3][:, 0:PAIRS], s1: weight[s3][:, 0:PAIRS], s2: swing[s3][:, 0:PAIRS], s3: weight[s3][:, 0:PAIRS]}
        top = {t: held("top%d" % t, [P, PAIRS], F32)[:] for t in (s1, s2, s3)}
        top[s0] = wo_raw[:, 0, 0:PAIRS]
        scaled_b = {t: held("scaled_b%d" % t, [P, PAIRS], F32)[:] for t in (s3,)}
        scaled_b[s0] = fix_raw[0][:, 0, 0:PAIRS]
        scaled_b[s1] = fix_raw[1][:, 0, 0:PAIRS]

        def count_turns(t, j0=0, j1=S):
            shifted = ring.tile([P, j1 - j0], U32, name="shifted")
            nc.scalar.activation(shifted[:], swing_ps[t, j0][:], ACT.Copy, bias=ROUNDER, scale=1.0 / TWO_PI)
            nc.scalar.activation(turns[t][:, j0:j1], shifted[:], ACT.Copy, bias=-ROUNDER, scale=1.0)

        def reduce_angle(t, j0=0, j1=S):
            angle[t, j0] = ring.tile([P, j1 - j0], F32, name="angle")
            nc.vector.scalar_tensor_tensor(angle[t, j0][:], turns[t][:, j0:j1], -TWO_PI, swing_ps[t, j0][:],
                                           ALU.mult, ALU.add)

        def sine(t, j0=0, j1=S):
            nc.scalar.activation(swing[t][:, j0:j1], angle[t, j0][:], ACT.Sin)

        def weigh(t):
            nc.scalar.activation(weight[t], wg_raw[:, t * S : (t + 1) * S], ACT.Copy, scale=gain_t[:, t : t + 1])

        def add_parts(t, j0=0, j1=S):
            nc.vector.tensor_tensor(form[t, j0], level[t][:, j0:j1], swing[t][:, j0:j1], ALU.add)

        def put_form(t, j0=0, j1=S):
            nc.vector.tensor_tensor(page[t][:].indirect(place[:, j0 // 16 : j1 // 16]), form[t, j0],
                                    weight[t][:, j0:j1], ALU.mult)

        def fetch_left(t):
            nc.vector.tensor_copy(a_t[t], page[t][:].indirect(left[:]))

        def fetch_right(t):
            nc.vector.tensor_copy(b_t[t], page[t][:].indirect(right[:]))
            if t == s2:
                scaled_b[t] = held("scaled_b%d" % t, [P, PAIRS], F32, tag="page%d" % s0)[:]
            nc.scalar.activation(scaled_b[t], b_t[t], ACT.Copy, scale=swap_t[:, t : t + 1])

        def larger(t):
            nc.vector.tensor_tensor(top[t], a_t[t], b_t[t], ALU.max)

        def put_left(t):
            nc.vector.tensor_copy(page[t][:].indirect(left[:]), top[t])

        def put_right(t):
            nc.vector.tensor_tensor(page[t][:].indirect(right[:]), a_t[t], scaled_b[t], ALU.add)


        def weave_page(copy, t, q):
            copy(out=page_b[q][:].rearrange("p (c j) -> p c j", j=PACK)[:, :, t], in_=page[t][:, q * QUARTER : (q + 1) * QUARTER])

        def weave(grouped, raw):
            nc.scalar.copy(out=grouped[:].rearrange("p (c i j) -> p c j i", i=4, j=PACK),
                           in_=raw[:].rearrange("p j (c i) -> p c j i", i=4))

        wo_b = held("wo_b", [P, PACK * N], BF16)
        wo_w = held("wo_w", [P, N], U32)
        wo_s = held("wo_s", [P, N], U8)
        fix_b = [held("fix_b%d" % h, [P, PACK * T2 // 2], BF16) for h in range(2)]
        fix_s = [held("fix_s%d" % h, [P, T2 // 2], U8) for h in range(2)]
        page_w = [held("page_w%d" % q, [P, QUARTER], U32) for q in range(4)]
        page_s = [held("page_s%d" % q, [P, QUARTER], U8) for q in range(4)]
        score_ps = {}

        def fixture_passes(h):
            for q in (2 * h, 2 * h + 1):
                cols = slice((q % 2) * QUARTER, (q % 2 + 1) * QUARTER)
                for pair in range(2):
                    score_ps[q, pair] = bank(2 * q + pair, [P, 2, QUARTER], "score_ps%d_%d" % (q, pair))
                    for i in range(2):
                        n0 = (2 * pair + i) * P
                        nc.tensor.matmul_mx(out=score_ps[q, pair][:, i, :], lhsT=wf_w[:, n0 : n0 + P].bitcast(FP8X4),
                                            lhsT_scale=wf_s[:].bitcast(U8)[:, n0 : n0 + P],
                                            rhs=fix_w[h][:, cols].bitcast(FP8X4), rhs_scale=fix_s[h][:, cols],
                                            start=(i == 0), stop=False)

        out_v = out.rearrange("(n p) c -> p n c", p=P)

        def page_passes(q):
            for pair in range(2):
                for i in range(2):
                    n0 = (2 * pair + i) * P
                    nc.tensor.matmul_mx(out=score_ps[q, pair][:, i, :], lhsT=wo_w[:, n0 : n0 + P].bitcast(FP8X4),
                                        lhsT_scale=wo_s[:, n0 : n0 + P], rhs=page_w[q][:].bitcast(FP8X4),
                                        rhs_scale=page_s[q][:], start=False, stop=(i == 1))

        def store(copy, q, pair):
            score = held("score%d_%d" % (q, pair), [P, 2, QUARTER], F32)
            copy(out=score[:], in_=score_ps[q, pair][:])
            nc.sync.dma_start(out_v[:, 2 * pair : 2 * pair + 2, q * QUARTER : (q + 1) * QUARTER], score[:])

        def quantise_fixtures(h, tag):
            fix_w[h] = held("fix_w%d" % h, [P, T2 // 2], U32, tag=tag)
            quantise(fix_w[h][:], fix_s[h][:], fix_b[h][:])
            fixture_passes(h)

        count_turns(s0, 0, half)
        squash(s0, 0, half)
        reduce_angle(s0, 0, half)
        count_turns(s0, half, S)
        sine(s0, 0, half)
        squash(s0, half, S)
        first_products(0, s3)
        reduce_angle(s0, half, S)
        nc.vector.tensor_scalar(weight[s0], wg_raw[:, s0 * S : (s0 + 1) * S], gain_t[:, s0 : s0 + 1], None, ALU.mult)
        add_parts(s0, 0, half)
        count_turns(s1)
        sine(s0, half, S)
        put_form(s0, 0, half)
        reduce_angle(s1)
        add_parts(s0, half, S)
        put_form(s0, half, S)
        for t, after in ((s1, s2), (s2, s3)):
            sine(t)
            count_turns(after)
            squash(t)
            weigh(t)
            reduce_angle(after)
            add_parts(t)
            put_form(t)
        sine(s3)
        squash(s3)
        weigh(s3)
        weave(wo_b, wo_raw)
        weave(fix_b[0], fix_raw[0])
        weave(fix_b[1], fix_raw[1])
        add_parts(s3)
        fetch_left(s0)
        fetch_right(s0)
        put_form(s3)
        fetch_left(s1)
        larger(s0)
        fetch_right(s1)
        put_left(s0)
        larger(s1)
        quantise(wo_w[:], wo_s[:], wo_b[:])
        put_right(s0)
        for q in range(4):
            weave_page(nc.scalar.copy, s0, q)
        put_right(s1)
        fetch_left(s2)
        put_left(s1)
        fetch_right(s2)
        fetch_left(s3)
        larger(s2)
        fetch_right(s3)
        put_left(s2)
        larger(s3)
        for q in range(4):
            weave_page(nc.scalar.copy, s1, q)
        put_right(s2)
        for q in range(4):
            weave_page(nc.scalar.copy, s2, q)
        quantise_fixtures(0, "top%d" % s2)
        put_left(s3)
        quantise_fixtures(1, "page%d" % s0)
        put_right(s3)

        def quantise_page(q):
            quantise(page_w[q][:], page_s[q][:], page_b[q][:])
            page_passes(q)

        weave_page(nc.vector.tensor_copy, s3, 0)
        weave_page(nc.scalar.copy, s3, 1)
        weave_page(nc.vector.tensor_copy, s3, 2)
        weave_page(nc.scalar.copy, s3, 3)
        for q in (0, 2, 1, 3):
            quantise_page(q)
        for q in (0, 2, 1, 3):
            store(nc.scalar.copy, q, 0)
            store(nc.scalar.copy if q == 0 else nc.vector.tensor_copy, q, 1)
